import numpy as np
import ml_dtypes


def mxq(x, axis, fmt="e4m3"):
    dtype, down = {"e4m3": (ml_dtypes.float8_e4m3fn, 7), "e5m2": (ml_dtypes.float8_e5m2, 14)}[fmt]
    v = np.moveaxis(np.asarray(x, np.float32).astype(ml_dtypes.bfloat16).astype(np.float64), axis, -1)
    blocks = v.reshape(v.shape[:-1] + (-1, 32))
    amax = np.abs(blocks).max(-1, keepdims=True)
    byte = np.maximum(np.where(amax > 0, np.frexp(amax)[1] - 1 + 127, 0) - down, 1)
    scale = np.exp2(byte - 127.0)
    codes = (blocks / scale).astype(np.float32).astype(dtype).astype(np.float64)
    return np.moveaxis((codes * scale).reshape(v.shape), -1, axis)


WIDE = False


def mx_kscale(k):
    if not WIDE:
        return np.ones(k)
    levels = np.array([10, -10, 5, -5, 0])
    if k % 512:
        return np.exp2(np.random.permutation(np.resize(levels, k // 32))).repeat(32)
    a = np.empty((k // 512, 16))
    for p in range(k // 512):
        a[p, :8] = np.random.permutation(np.resize(levels, 8))
        for g in range(8):
            far = levels[np.abs(levels - a[p, g]) >= 10]
            a[p, g + 8] = far[np.random.randint(len(far))]
    return np.exp2(a.ravel()).repeat(32)


def f64(x):
    return np.asarray(x).astype(np.float64)


def striped(idx):
    return np.tile(idx.reshape(-1, 16).T, (8, 1)).astype(np.uint16)


def unstriped(offs):
    return offs[:16].T.reshape(-1).astype(np.int64)


def striped8(idx):
    return np.concatenate([x.reshape(-1, 16).T for x in idx]).astype(np.uint16)


def runs(offs, k):
    lists = np.stack([offs[16 * r : 16 * r + 16].T.reshape(-1) for r in range(8)]).astype(np.int64)
    return lists[np.arange(k) % 512 // 64]


def pack_weight(w):
    k, n = w.shape
    w = f64(np.asarray(w, np.float32).astype(ml_dtypes.bfloat16)).reshape(k // 32, 32, n)
    amax = np.abs(w).max(1)
    byte = np.clip(np.where(amax > 0, np.frexp(amax)[1] - 1 + 127 - 7, 1), 1, 254)
    scaled = (w * np.exp2(127.0 - byte)[:, None, :]).reshape(k, n).astype(np.float32)
    words = np.ascontiguousarray(scaled.reshape(k // 512, 128, 4, n).transpose(0, 1, 3, 2)).astype(ml_dtypes.float8_e4m3fn).view(np.uint8)
    return words, np.ascontiguousarray(byte.astype(np.uint8).reshape(k // 512, 16, n))


def unpack_weight(words, scales):
    g, p, n, _ = words.shape
    vals = np.ascontiguousarray(words).view(ml_dtypes.float8_e4m3fn).astype(np.float64) * np.repeat(np.exp2(scales.astype(np.float64) - 127.0), 8, axis=1)[..., None]
    return vals.transpose(0, 1, 3, 2).reshape(g * 512, n)

def planes(y):
    n, m = y.shape
    v = y.astype(np.float32).astype(ml_dtypes.bfloat16).astype(np.float64).reshape(n // 32, 32, m)
    top = np.abs(v).max(1)
    byte = np.clip(np.where(top > 0, np.frexp(top)[1] - 1 + 127 - 7, 1), 1, 254)
    codes = (v * np.exp2(127.0 - byte)[:, None, :]).reshape(n, m).astype(np.float32).astype(ml_dtypes.float8_e4m3fn).view(np.uint8)
    words = codes.reshape(n // 512, 128, 4, m).transpose(0, 1, 3, 2)
    return np.ascontiguousarray(words), np.ascontiguousarray(byte.astype(np.uint8).reshape(n // 512, 16, m))


K, T, S, N, H = 512, 2048, 512, 512, 512


def setup_inputs():
    n = np.random.standard_normal
    s = mx_kscale(K)[:, None]
    u = mx_kscale(H)
    packed_xT = pack_weight(n((K, T)) * s)
    packed_w1 = pack_weight(n((K, H)) / np.sqrt(K) / s)
    packed_w2 = pack_weight(n((H, N)) / np.sqrt(2 * H) / u[:, None])
    packed_w3 = pack_weight(n((K, N)) / np.sqrt(2 * K) / s)
    return {
        "x_words": packed_xT[0],
        "x_scales": packed_xT[1],
        "w1_words": packed_w1[0],
        "w1_scales": packed_w1[1],
        "gn": (np.random.uniform(0.5, 1.5, (H, 1)) * u[:, None]).astype(np.float32),
        "w2_words": packed_w2[0],
        "w2_scales": packed_w2[1],
        "w3_words": packed_w3[0],
        "w3_scales": packed_w3[1],
        "offs": striped(np.random.permutation(T)[:S]),
        "n1": striped(np.random.permutation(S)),
        "hz": striped8(np.random.randint(0, T, (8, S))),
        "n2": striped(np.random.permutation(S)),
        "n3": striped(np.random.permutation(S)),
    }


def reference(x_words, x_scales, w1_words, w1_scales, gn, w2_words, w2_scales, w3_words, w3_scales, offs, n1, hz, n2, n3):
    xq = unpack_weight(x_words, x_scales)[:, unstriped(offs)]
    y = unpack_weight(w1_words, w1_scales).T @ xq
    z = f64(gn) * (y / (np.abs(y[:, unstriped(n1)]) + 0.5))
    x_hz = unpack_weight(x_words, x_scales)[np.arange(K)[:, None], runs(hz, K)]
    h = unpack_weight(w2_words, w2_scales).T @ mxq(z, 0, "e4m3") + unpack_weight(w3_words, w3_scales).T @ x_hz
    pa = h[:, unstriped(n2)]
    kr = np.exp(-0.5 * ((h - pa) ** 2))
    pb = h[:, unstriped(n3)]
    kr2 = np.exp(-0.5 * ((h - pb) ** 2))
    out_0 = (kr * pa + kr2 * pb) / (kr + kr2 + 0.5)
    return (out_0,) + planes(out_0)

@@ -1,0 +1,285 @@
+from contextlib import ExitStack
+
+import concourse.mybir as mybir
+
+FLOPS = 805306368
+
+F32 = mybir.dt.float32
+BF16 = mybir.dt.bfloat16
+I32 = mybir.dt.int32
+U32 = mybir.dt.uint32
+U16 = mybir.dt.uint16
+U8 = mybir.dt.uint8
+FP8X4 = mybir.dt.float8_e4m3fn_x4
+ACT = mybir.ActivationFunctionType
+ALU = mybir.AluOpType
+
+P = 128
+PACK = 4
+T = 2048
+S = 512
+CH = 128
+NCH = S // CH
+HALF = 256
+
+
+def tile_picked_mixhnormkern_none_po_kernel(
+    tc, x_words, x_scales, w1_words, w1_scales, gn, w2_words, w2_scales, w3_words, w3_scales,
+    offs, n1, hz, n2, n3, out_0, out_1, out_2,
+):
+    nc = tc.nc
+    with ExitStack() as ctx:
+        sb = ctx.enter_context(tc.tile_pool(name="sb", bufs=1))
+        ps = ctx.enter_context(tc.psum_pool(name="ps", bufs=1))
+
+        def words_of(dram):
+            return dram[0].rearrange("p n t -> p (n t)").bitcast(I32)
+
+        def scale_rows(dram, q):
+            return dram[0, 4 * q : 4 * q + 4, :].bitcast(I32)
+
+        def load_list(dram, name):
+            lst = sb.tile([P, S // 16], U16, name=name)
+            nc.sync.dma_start(lst[:], dram)
+            return lst
+
+        def entries(lst, start, count):
+            return lst[:, start // 16 : (start + count) // 16]
+
+        offs_l = load_list(offs, "offs_l")
+        hz_l = load_list(hz, "hz_l")
+        xs = sb.tile([P, T], U8, name="xs", align_bytes=64)
+        for q in range(4):
+            nc.sync.dma_start(xs[32 * q : 32 * q + 32, :].bitcast(I32), scale_rows(x_scales, q).partition_broadcast(8))
+        xw = sb.tile([P, T], U32, name="xw", align_bytes=64)
+        nc.sync.dma_start(xw[:].bitcast(I32), words_of(x_words))
+        w1_raw = sb.tile([P, S], U32, name="w1_raw", align_bytes=64)
+        nc.sync.dma_start(w1_raw[:].bitcast(I32), words_of(w1_words))
+        s1_raw = sb.tile([P, S], U8, name="s1_raw", align_bytes=64)
+        for q in range(4):
+            nc.gpsimd.dma_start(s1_raw[32 * q : 32 * q + 32, :].bitcast(I32), scale_rows(w1_scales, q).partition_broadcast(8))
+
+        gain = sb.tile([P, PACK], F32, name="gain")
+        nc.sync.dma_start(gain[:], gn.rearrange("(p t) o -> p (t o)", t=PACK))
+        n1_l = load_list(n1, "n1_l")
+        w3_raw = sb.tile([P, S], U32, name="w3_raw", align_bytes=64)
+        nc.sync.dma_start(w3_raw[:].bitcast(I32), words_of(w3_words))
+        w2_raw = sb.tile([P, S], U32, name="w2_raw", align_bytes=64)
+        nc.sync.dma_start(w2_raw[:].bitcast(I32), words_of(w2_words))
+        s23_raw = sb.tile([P, S], U8, name="s23_raw", align_bytes=64)
+        nc.gpsimd.memset(s23_raw[:].bitcast(I32), 0)
+        for q in range(4):
+            nc.sync.dma_start(s23_raw[32 * q : 32 * q + 4, :].bitcast(I32), scale_rows(w2_scales, q))
+            nc.sync.dma_start(s23_raw[32 * q + 4 : 32 * q + 8, :].bitcast(I32), scale_rows(w3_scales, q))
+        n2_l = load_list(n2, "n2_l")
+        n3_l = load_list(n3, "n3_l")
+
+        def deal(engine_copy, raw, dtype, name):
+            dealt = sb.tile([P, S], dtype, name=name, align_bytes=64)
+            engine_copy(dealt[:].rearrange("p (t m) -> p t m", t=PACK), raw[:].rearrange("p (m t) -> p t m", t=PACK))
+            return dealt
+
+        gs = sb.tile([P, S], U8, name="gs", align_bytes=64)
+        nc.vector.tensor_copy(gs[:], xs[:].indirect(offs_l[:]))
+        hs_raw = sb.tile([P, S], U8, name="hs_raw", align_bytes=64)
+        nc.vector.tensor_copy(hs_raw[:], xs[:].indirect(hz_l[:]))
+        w1 = deal(nc.scalar.copy, w1_raw, U32, "w1")
+        s1 = deal(nc.gpsimd.tensor_copy, s1_raw, U8, "s1")
+        gw = sb.tile([P, S], U32, name="gw", align_bytes=64)
+        for c in range(NCH):
+            nc.vector.tensor_copy(gw[:, c * CH : (c + 1) * CH], xw[:].indirect(entries(offs_l, c * CH, CH)))
+
+        hw = sb.tile([P, S], U32, name="hw", align_bytes=64)
+        nc.vector.tensor_copy(hw[:], xw[:].indirect(hz_l[:]))
+        hs = sb.tile([P, S], U8, name="hs", align_bytes=64)
+        nc.gpsimd.memset(hs[:].bitcast(I32), 0)
+        for r in range(4):
+            src = r + 16 * (r // 2)
+            nc.sync.dma_start(hs[r:P:32, :].bitcast(I32), hs_raw[src:P:32, :].bitcast(I32))
+
+        y_ps = [ps.tile([P, PACK, CH], F32, name="y%d" % c) for c in range(NCH)]
+        mag = sb.tile([P, PACK, S], F32, name="mag")
+        root = sb.tile([P, PACK, S], F32, name="root")
+        fac = [sb.tile([P, S], F32, name="fac%d" % t) for t in range(PACK)]
+        for c in range(NCH):
+            cols = slice(c * CH, (c + 1) * CH)
+            for t in range(PACK):
+                nc.tensor.matmul_mx(
+                    y_ps[c][:, t, :], lhsT=w1[:, t * P : (t + 1) * P].bitcast(FP8X4), lhsT_scale=s1[:, t * P : (t + 1) * P],
+                    rhs=gw[:, cols].bitcast(FP8X4), rhs_scale=gs[:, cols], start=True, stop=True,
+                )
+            nc.scalar.activation(mag[:, :, cols], y_ps[c][:], ACT.Abs)
+            if c == 1:
+                half = slice(0, HALF)
+                nc.scalar.activation(root[:, :, half], mag[:, :, half], ACT.Abs_reciprocal_sqrt, bias=0.5)
+                for t in range(PACK):
+                    nc.vector.scalar_tensor_tensor(
+                        fac[t][:, half], root[:, t, half], gain[:, t : t + 1], root[:, t, half], ALU.mult, ALU.mult
+                    )
+        half = slice(HALF, S)
+        for t in range(PACK):
+            nc.scalar.activation(root[:, t, half], mag[:, t, half], ACT.Abs_reciprocal_sqrt, bias=0.5)
+            nc.vector.scalar_tensor_tensor(
+                fac[t][:, half], root[:, t, half], gain[:, t : t + 1], root[:, t, half], ALU.mult, ALU.mult
+            )
+
+        w3 = deal(nc.vector.tensor_copy, w3_raw, U32, "w3")
+        s23 = deal(nc.vector.tensor_copy, s23_raw, U8, "s23")
+        w2 = deal(nc.vector.tensor_copy, w2_raw, U32, "w2")
+
+        h_ps = [ps.tile([P, S], F32, name="h%d" % t) for t in range(PACK)]
+        for t in range(PACK):
+            nc.tensor.matmul_mx(
+                h_ps[t][:], lhsT=w3[:, t * P : (t + 1) * P].bitcast(FP8X4), lhsT_scale=s23[4:P, t * P : (t + 1) * P],
+                rhs=hw[:].bitcast(FP8X4), rhs_scale=hs[:], start=True, stop=False,
+            )
+
+        got = sb.tile([P, PACK, S], F32, name="got")
+        zb = sb.tile([P, PACK, S], BF16, name="zb")
+        zi = sb.tile([P, S, PACK], BF16, name="zi", align_bytes=64)
+        zq = sb.tile([P, S], U32, name="zq", align_bytes=64)
+        zs = sb.tile([P, S], U8, name="zs", align_bytes=64)
+
+        def chunk(c):
+            return slice(c * CH, (c + 1) * CH)
+
+        def z_mul(c):
+            nc.vector.tensor_tensor(zb[:, :, chunk(c)], y_ps[c][:], got[:, :, chunk(c)], ALU.mult)
+
+        def z_weave(c):
+            nc.vector.tensor_copy(
+                zi[:, chunk(c), :].rearrange("p (c i) t -> p c t i", i=4), zb[:, :, chunk(c)].rearrange("p t (c i) -> p c t i", i=4)
+            )
+
+        def z_quant(c):
+            cols = chunk(c)
+            nc.vector.quantize_mx(zq[:, cols].bitcast(FP8X4), zs[:, cols], zi[:, cols, :].rearrange("p j t -> p (j t)"))
+            for t in range(PACK):
+                nc.tensor.matmul_mx(
+                    h_ps[t][:, cols], lhsT=w2[:, t * P : (t + 1) * P].bitcast(FP8X4), lhsT_scale=s23[:, t * P : (t + 1) * P],
+                    rhs=zq[:, cols].bitcast(FP8X4), rhs_scale=zs[:, cols], start=False, stop=(c == NCH - 1),
+                )
+
+        for start, count in ((0, 256), (256, 128), (384, 128)):
+            for t in range(PACK):
+                nc.scalar.activation(got[:, t, start : start + count], fac[t][:].indirect(entries(n1_l, start, count)), ACT.Copy)
+
+        z_mul(0)
+        z_mul(1)
+        z_weave(0)
+        z_weave(1)
+        z_quant(0)
+        z_mul(2)
+        z_quant(1)
+        z_weave(2)
+        z_mul(3)
+        z_quant(2)
+        z_weave(3)
+        z_quant(3)
+
+        h = [sb.tile([P, S], F32, name="hrow%d" % t) for t in range(PACK)]
+        near = sb.tile([P, PACK, 2, S], F32, name="near")
+        dif = sb.tile([P, PACK, 2, S], F32, name="dif")
+        sq = sb.tile([P, PACK, 2, S], F32, name="sq")
+        kr = sb.tile([P, PACK, 2, S], F32, name="kr")
+        prod = sb.tile([P, PACK, 2, S], F32, name="prod")
+        ksum = sb.tile([P, PACK, S], F32, name="ksum")
+        num = sb.tile([P, PACK, S], F32, name="num")
+        for t in range(PACK):
+            nc.vector.tensor_copy(h[t][:], h_ps[t][:])
+
+        def fetch(t):
+            for a, lst in enumerate((n2_l, n3_l)):
+                for start in range(0, S, HALF):
+                    nc.scalar.activation(near[:, t, a, start : start + HALF], h[t][:].indirect(entries(lst, start, HALF)), ACT.Copy)
+
+        def sub(t, a):
+            nc.vector.tensor_tensor(dif[:, t, a, :], near[:, t, a, :], h_ps[t][:], ALU.subtract)
+
+        def square(t):
+            nc.vector.tensor_tensor(sq[:, t, :, :], dif[:, t, :, :], dif[:, t, :, :], ALU.mult)
+
+        def expo(t):
+            nc.scalar.activation(kr[:, t, :, :], sq[:, t, :, :], ACT.Exp, scale=-0.5)
+
+        def ksums(t):
+            nc.vector.tensor_tensor(ksum[:, t, :], kr[:, t, 0, :], kr[:, t, 1, :], ALU.add)
+
+        def prods(t):
+            nc.vector.tensor_tensor(prod[:, t, :, :], kr[:, t, :, :], near[:, t, :, :], ALU.mult)
+
+        def nums(t):
+            nc.vector.tensor_tensor(num[:, t, :], prod[:, t, 0, :], prod[:, t, 1, :], ALU.add)
+
+        fetch(0)
+        sub(0, 0)
+        sub(0, 1)
+        fetch(1)
+        square(0)
+        expo(0)
+        sub(1, 0)
+        sub(1, 1)
+        fetch(2)
+        ksums(0)
+        square(1)
+        expo(1)
+        sub(2, 0)
+        prods(0)
+        sub(2, 1)
+        fetch(3)
+        ksums(1)
+        square(2)
+        expo(2)
+        sub(3, 0)
+        nums(0)
+        sub(3, 1)
+        for a in range(2):
+            nc.scalar.activation(sq[:, 3, a, :], dif[:, 3, a, :], ACT.Square)
+        expo(3)
+        prods(1)
+        ksums(2)
+        nums(1)
+        prods(2)
+        ksums(3)
+        nums(2)
+        prods(3)
+        nums(3)
+
+        root2 = sb.tile([P, PACK, S], F32, name="root2")
+        rec = sb.tile([P, PACK, S], F32, name="rec")
+        res = sb.tile([P, PACK, S], F32, name="res")
+        ri = sb.tile([P, S, PACK], BF16, name="ri", align_bytes=64)
+        oq = sb.tile([P, S], U32, name="oq", align_bytes=64)
+        osc = sb.tile([P, S], U8, name="osc", align_bytes=64)
+        out_rows = out_0.rearrange("(p t) j -> p t j", t=PACK)
+        out_words = words_of(out_1)
+        pieces = [slice(0, 128), slice(128, 256), slice(256, 384), slice(384, 448), slice(448, 512)]
+
+        def o_rec(cols):
+            nc.scalar.activation(root2[:, :, cols], ksum[:, :, cols], ACT.Abs_reciprocal_sqrt, bias=0.5)
+            nc.scalar.activation(rec[:, :, cols], root2[:, :, cols], ACT.Square)
+
+        def o_mul(cols):
+            nc.vector.tensor_tensor(res[:, :, cols], num[:, :, cols], rec[:, :, cols], ALU.mult)
+            nc.sync.dma_start(out_rows[:, :, cols], res[:, :, cols])
+
+        def o_weave(cols):
+            nc.vector.tensor_copy(
+                ri[:, cols, :].rearrange("p (c i) t -> p c t i", i=4), res[:, :, cols].rearrange("p t (c i) -> p c t i", i=4)
+            )
+
+        def o_quant(cols):
+            nc.vector.quantize_mx(oq[:, cols].bitcast(FP8X4), osc[:, cols], ri[:, cols, :].rearrange("p j t -> p (j t)"))
+            nc.sync.dma_start(out_words[:, cols], oq[:, cols].bitcast(I32))
+
+        for cols in pieces:
+            o_rec(cols)
+        for i in range(len(pieces) + 2):
+            if i < len(pieces):
+                o_mul(pieces[i])
+            if 2 <= i:
+                o_quant(pieces[i - 2])
+            if 1 <= i <= len(pieces):
+                o_weave(pieces[i - 1])
+        for q in range(4):
+            nc.scalar.dma_start(scale_rows(out_2, q), osc[32 * q : 32 * q + 4, :].bitcast(I32))

@@ -1,6 +1,7 @@
 from contextlib import ExitStack
 
 import concourse.mybir as mybir
+from concourse.masks import make_identity
 
 FLOPS = 805306368
 
@@ -47,30 +48,33 @@ def tile_picked_mixhnormkern_none_po_kernel(
             return lst[:, start // 16 : (start + count) // 16]
 
         offs_l = load_list(offs, "offs_l")
-        hz_l = load_list(hz, "hz_l")
+        s1_raw = sb.tile([P, S], U8, name="s1_raw", align_bytes=64)
+        nc.sync.dma_start(s1_raw[:].bitcast(I32), w1_scales[0].bitcast(I32).unsqueeze(1).to_broadcast([16, 8, S // 4]))
         xs = sb.tile([P, T], U8, name="xs", align_bytes=64)
         for q in range(4):
             nc.sync.dma_start(xs[32 * q : 32 * q + 32, :].bitcast(I32), scale_rows(x_scales, q).partition_broadcast(8))
-        xw = sb.tile([P, T], U32, name="xw", align_bytes=64)
-        nc.sync.dma_start(xw[:].bitcast(I32), words_of(x_words))
         w1_raw = sb.tile([P, S], U32, name="w1_raw", align_bytes=64)
         nc.sync.dma_start(w1_raw[:].bitcast(I32), words_of(w1_words))
-        s1_raw = sb.tile([P, S], U8, name="s1_raw", align_bytes=64)
-        for q in range(4):
-            nc.gpsimd.dma_start(s1_raw[32 * q : 32 * q + 32, :].bitcast(I32), scale_rows(w1_scales, q).partition_broadcast(8))
+        xw = sb.tile([P, T], U32, name="xw", align_bytes=64)
+        nc.sync.dma_start(xw[:].bitcast(I32), words_of(x_words))
+        one = sb.tile([P, 1], F32, name="one")
+        nc.gpsimd.memset(one[:], 1.0)
+        warm = sb.tile([P, 2], F32, name="warm")
+        nc.scalar.activation(warm[:, 0:1], one[:], ACT.Abs_reciprocal_sqrt)
 
+        hz_l = load_list(hz, "hz_l")
         gain = sb.tile([P, PACK], F32, name="gain")
         nc.sync.dma_start(gain[:], gn.rearrange("(p t) o -> p (t o)", t=PACK))
         n1_l = load_list(n1, "n1_l")
-        w3_raw = sb.tile([P, S], U32, name="w3_raw", align_bytes=64)
-        nc.sync.dma_start(w3_raw[:].bitcast(I32), words_of(w3_words))
-        w2_raw = sb.tile([P, S], U32, name="w2_raw", align_bytes=64)
-        nc.sync.dma_start(w2_raw[:].bitcast(I32), words_of(w2_words))
         s23_raw = sb.tile([P, S], U8, name="s23_raw", align_bytes=64)
         nc.gpsimd.memset(s23_raw[:].bitcast(I32), 0)
         for q in range(4):
             nc.sync.dma_start(s23_raw[32 * q : 32 * q + 4, :].bitcast(I32), scale_rows(w2_scales, q))
             nc.sync.dma_start(s23_raw[32 * q + 4 : 32 * q + 8, :].bitcast(I32), scale_rows(w3_scales, q))
+        w3_raw = sb.tile([P, S], U32, name="w3_raw", align_bytes=64)
+        nc.sync.dma_start(w3_raw[:].bitcast(I32), words_of(w3_words))
+        w2_raw = sb.tile([P, S], U32, name="w2_raw", align_bytes=64)
+        nc.sync.dma_start(w2_raw[:].bitcast(I32), words_of(w2_words))
         n2_l = load_list(n2, "n2_l")
         n3_l = load_list(n3, "n3_l")
 
@@ -79,23 +83,27 @@ def tile_picked_mixhnormkern_none_po_kernel(
             engine_copy(dealt[:].rearrange("p (t m) -> p t m", t=PACK), raw[:].rearrange("p (m t) -> p t m", t=PACK))
             return dealt
 
+        s1_dealt = deal(nc.vector.tensor_copy, s1_raw, U8, "s1_dealt")
+        s1 = sb.tile([P, S], U8, name="s1", align_bytes=64)
+        for r in range(4):
+            nc.scalar.dma_start(s1[r:P:32, :].bitcast(I32), s1_dealt[8 * r : P : 32, :].bitcast(I32))
+        ident = sb.tile([P, P], F32, name="ident")
+        make_identity(nc, ident[:])
         gs = sb.tile([P, S], U8, name="gs", align_bytes=64)
         nc.vector.tensor_copy(gs[:], xs[:].indirect(offs_l[:]))
-        hs_raw = sb.tile([P, S], U8, name="hs_raw", align_bytes=64)
-        nc.vector.tensor_copy(hs_raw[:], xs[:].indirect(hz_l[:]))
         w1 = deal(nc.scalar.copy, w1_raw, U32, "w1")
-        s1 = deal(nc.gpsimd.tensor_copy, s1_raw, U8, "s1")
         gw = sb.tile([P, S], U32, name="gw", align_bytes=64)
         for c in range(NCH):
             nc.vector.tensor_copy(gw[:, c * CH : (c + 1) * CH], xw[:].indirect(entries(offs_l, c * CH, CH)))
 
         hw = sb.tile([P, S], U32, name="hw", align_bytes=64)
+        hs_raw = sb.tile([P, S], U8, name="hs_raw", align_bytes=64)
+        nc.vector.tensor_copy(hs_raw[:], xs[:].indirect(hz_l[:]))
         nc.vector.tensor_copy(hw[:], xw[:].indirect(hz_l[:]))
         hs = sb.tile([P, S], U8, name="hs", align_bytes=64)
-        nc.gpsimd.memset(hs[:].bitcast(I32), 0)
-        for r in range(4):
-            src = r + 16 * (r // 2)
-            nc.sync.dma_start(hs[r:P:32, :].bitcast(I32), hs_raw[src:P:32, :].bitcast(I32))
+        nc.vector.tensor_copy(hs[:].bitcast(I32), hs_raw[:].bitcast(I32))
+        for r in (2, 3):
+            nc.sync.dma_start(hs[r:P:32, :].bitcast(I32), hs_raw[16 + r : P : 32, :].bitcast(I32))
 
         y_ps = [ps.tile([P, PACK, CH], F32, name="y%d" % c) for c in range(NCH)]
         mag = sb.tile([P, PACK, S], F32, name="mag")
@@ -123,9 +131,9 @@ def tile_picked_mixhnormkern_none_po_kernel(
                 fac[t][:, half], root[:, t, half], gain[:, t : t + 1], root[:, t, half], ALU.mult, ALU.mult
             )
 
-        w3 = deal(nc.vector.tensor_copy, w3_raw, U32, "w3")
-        s23 = deal(nc.vector.tensor_copy, s23_raw, U8, "s23")
-        w2 = deal(nc.vector.tensor_copy, w2_raw, U32, "w2")
+        w3 = deal(nc.gpsimd.tensor_copy, w3_raw, U32, "w3")
+        s23 = deal(nc.gpsimd.tensor_copy, s23_raw, U8, "s23")
+        w2 = deal(nc.gpsimd.tensor_copy, w2_raw, U32, "w2")
 
         h_ps = [ps.tile([P, S], F32, name="h%d" % t) for t in range(PACK)]
         for t in range(PACK):
@@ -134,9 +142,10 @@ def tile_picked_mixhnormkern_none_po_kernel(
                 rhs=hw[:].bitcast(FP8X4), rhs_scale=hs[:], start=True, stop=False,
             )
 
-        got = sb.tile([P, PACK, S], F32, name="got")
-        zb = sb.tile([P, PACK, S], BF16, name="zb")
-        zi = sb.tile([P, S, PACK], BF16, name="zi", align_bytes=64)
+        spans = ((0, 256), (256, 128), (384, 128))
+        got = [sb.tile([P, PACK, count], F32, name="got%d" % start) for start, count in spans]
+        got_of = [got[0][:, :, :CH], got[0][:, :, CH:], got[1][:], got[2][:]]
+        zi = [sb.tile([P, CH, PACK], BF16, name="zi%d" % c, align_bytes=64) for c in range(NCH)]
         zq = sb.tile([P, S], U32, name="zq", align_bytes=64)
         zs = sb.tile([P, S], U8, name="zs", align_bytes=64)
 
@@ -144,142 +153,182 @@ def tile_picked_mixhnormkern_none_po_kernel(
             return slice(c * CH, (c + 1) * CH)
 
         def z_mul(c):
-            nc.vector.tensor_tensor(zb[:, :, chunk(c)], y_ps[c][:], got[:, :, chunk(c)], ALU.mult)
-
-        def z_weave(c):
-            nc.vector.tensor_copy(
-                zi[:, chunk(c), :].rearrange("p (c i) t -> p c t i", i=4), zb[:, :, chunk(c)].rearrange("p t (c i) -> p c t i", i=4)
+            nc.vector.tensor_tensor(
+                zi[c][:].rearrange("p (c i) t -> p c t i", i=4),
+                y_ps[c][:].rearrange("p t (c i) -> p c t i", i=4),
+                got_of[c].rearrange("p t (c i) -> p c t i", i=4),
+                ALU.mult,
             )
 
         def z_quant(c):
             cols = chunk(c)
-            nc.vector.quantize_mx(zq[:, cols].bitcast(FP8X4), zs[:, cols], zi[:, cols, :].rearrange("p j t -> p (j t)"))
+            nc.vector.quantize_mx(zq[:, cols].bitcast(FP8X4), zs[:, cols], zi[c][:].rearrange("p j t -> p (j t)"))
             for t in range(PACK):
                 nc.tensor.matmul_mx(
                     h_ps[t][:, cols], lhsT=w2[:, t * P : (t + 1) * P].bitcast(FP8X4), lhsT_scale=s23[:, t * P : (t + 1) * P],
                     rhs=zq[:, cols].bitcast(FP8X4), rhs_scale=zs[:, cols], start=False, stop=(c == NCH - 1),
                 )
 
-        for start, count in ((0, 256), (256, 128), (384, 128)):
+        for dst, (start, count) in zip(got, spans):
             for t in range(PACK):
-                nc.scalar.activation(got[:, t, start : start + count], fac[t][:].indirect(entries(n1_l, start, count)), ACT.Copy)
+                nc.scalar.activation(dst[:, t, :], fac[t][:].indirect(entries(n1_l, start, count)), ACT.Copy)
+        nc.scalar.activation(warm[:, 1:2], got[2][:, PACK - 1, CH - 1 : CH], ACT.Tanh)
 
         z_mul(0)
         z_mul(1)
-        z_weave(0)
-        z_weave(1)
         z_quant(0)
         z_mul(2)
         z_quant(1)
-        z_weave(2)
         z_mul(3)
         z_quant(2)
-        z_weave(3)
         z_quant(3)
 
-        h = [sb.tile([P, S], F32, name="hrow%d" % t) for t in range(PACK)]
-        near = sb.tile([P, PACK, 2, S], F32, name="near")
+        h = [sb.tile([P, S + 16], F32, name="hrow%d" % t) for t in range(PACK)]
+        for t in range(PACK):
+            nc.gpsimd.memset(h[t][:, S:], 0.0)
         dif = sb.tile([P, PACK, 2, S], F32, name="dif")
-        sq = sb.tile([P, PACK, 2, S], F32, name="sq")
+        sq = [sb.tile([P, 2, S], F32, name="sq%d" % t) for t in range(PACK)]
+        near = [sb.tile([P, 2, S], F32, name="near%d" % t) for t in range(2)] + sq[:2]
         kr = sb.tile([P, PACK, 2, S], F32, name="kr")
         prod = sb.tile([P, PACK, 2, S], F32, name="prod")
-        ksum = sb.tile([P, PACK, S], F32, name="ksum")
         num = sb.tile([P, PACK, S], F32, name="num")
         for t in range(PACK):
-            nc.vector.tensor_copy(h[t][:], h_ps[t][:])
+            if t == 0:
+                nc.scalar.copy(h[t][:, :S], h_ps[t][:])
+            else:
+                nc.vector.tensor_copy(h[t][:, :S], h_ps[t][:])
 
         def fetch(t):
             for a, lst in enumerate((n2_l, n3_l)):
-                for start in range(0, S, HALF):
-                    nc.scalar.activation(near[:, t, a, start : start + HALF], h[t][:].indirect(entries(lst, start, HALF)), ACT.Copy)
+                nc.scalar.activation(near[t][:, a, :], h[t][:].indirect(lst[:]), ACT.Copy)
 
         def sub(t, a):
-            nc.vector.tensor_tensor(dif[:, t, a, :], near[:, t, a, :], h_ps[t][:], ALU.subtract)
+            nc.vector.tensor_tensor(dif[:, t, a, :], near[t][:, a, :], h_ps[t][:], ALU.subtract)
 
         def square(t):
-            nc.vector.tensor_tensor(sq[:, t, :, :], dif[:, t, :, :], dif[:, t, :, :], ALU.mult)
+            nc.vector.tensor_tensor(sq[t][:], dif[:, t, :, :], dif[:, t, :, :], ALU.mult)
 
         def expo(t):
-            nc.scalar.activation(kr[:, t, :, :], sq[:, t, :, :], ACT.Exp, scale=-0.5)
+            nc.scalar.activation(kr[:, t, :, :], sq[t][:], ACT.Exp, scale=-0.5)
 
         def ksums(t):
-            nc.vector.tensor_tensor(ksum[:, t, :], kr[:, t, 0, :], kr[:, t, 1, :], ALU.add)
+            for c in range(NCH):
+                for a in range(2):
+                    nc.tensor.matmul(y_ps[c][:, t, :], lhsT=kr[:, t, a, chunk(c)], rhs=ident[:], is_transpose=True, start=(a == 0), stop=(a == 1))
 
         def prods(t):
-            nc.vector.tensor_tensor(prod[:, t, :, :], kr[:, t, :, :], near[:, t, :, :], ALU.mult)
+            nc.vector.tensor_tensor(prod[:, t, :, :], kr[:, t, :, :], near[t][:], ALU.mult)
 
         def nums(t):
             nc.vector.tensor_tensor(num[:, t, :], prod[:, t, 0, :], prod[:, t, 1, :], ALU.add)
 
+        def half_square(t, a):
+            nc.vector.tensor_tensor(sq[t][:, a, :], dif[:, t, a, :], dif[:, t, a, :], ALU.mult)
+
+        def half_expo(t, a):
+            nc.scalar.activation(kr[:, t, a, :], sq[t][:, a, :], ACT.Exp, scale=-0.5)
+
         fetch(0)
         sub(0, 0)
+        half_square(0, 0)
         sub(0, 1)
+        half_square(0, 1)
         fetch(1)
-        square(0)
         expo(0)
+        ksums(0)
         sub(1, 0)
         sub(1, 1)
-        fetch(2)
-        ksums(0)
         square(1)
+        fetch(2)
         expo(1)
-        sub(2, 0)
-        prods(0)
-        sub(2, 1)
-        fetch(3)
         ksums(1)
+        prods(0)
+        sub(2, 0)
+        sub(2, 1)
         square(2)
+        fetch(3)
         expo(2)
-        sub(3, 0)
-        nums(0)
-        sub(3, 1)
-        for a in range(2):
-            nc.scalar.activation(sq[:, 3, a, :], dif[:, 3, a, :], ACT.Square)
-        expo(3)
-        prods(1)
         ksums(2)
-        nums(1)
-        prods(2)
+        sub(3, 0)
+        prods(1)
+        sub(3, 1)
+        half_square(3, 0)
+        half_square(3, 1)
+        half_expo(3, 0)
+        half_expo(3, 1)
         ksums(3)
-        nums(2)
+        nums(0)
+        prods(2)
+        nums(1)
         prods(3)
+        nums(2)
         nums(3)
 
-        root2 = sb.tile([P, PACK, S], F32, name="root2")
-        rec = sb.tile([P, PACK, S], F32, name="rec")
-        res = sb.tile([P, PACK, S], F32, name="res")
-        ri = sb.tile([P, S, PACK], BF16, name="ri", align_bytes=64)
+        root2 = sb.tile([P, NCH, PACK, P], F32, name="root2")
+        rec = sb.tile([P, NCH, PACK, P], F32, name="rec")
+        part = sb.tile([P, PACK, CH], F32, name="part")
+        res = [sb.tile([P, PACK, CH], F32, name="res%d" % c) for c in range(NCH)]
+        ri = [sb.tile([P, CH, PACK], BF16, name="ri%d" % c, align_bytes=64) for c in range(NCH)]
         oq = sb.tile([P, S], U32, name="oq", align_bytes=64)
         osc = sb.tile([P, S], U8, name="osc", align_bytes=64)
         out_rows = out_0.rearrange("(p t) j -> p t j", t=PACK)
         out_words = words_of(out_1)
-        pieces = [slice(0, 128), slice(128, 256), slice(256, 384), slice(384, 448), slice(448, 512)]
+        back = [h_ps[c][:].rearrange("p (t j) -> p t j", t=PACK) for c in range(NCH)]
 
-        def o_rec(cols):
-            nc.scalar.activation(root2[:, :, cols], ksum[:, :, cols], ACT.Abs_reciprocal_sqrt, bias=0.5)
-            nc.scalar.activation(rec[:, :, cols], root2[:, :, cols], ACT.Square)
+        def o_root(c, ts):
+            nc.scalar.activation(root2[:, c, ts, :], y_ps[c][:, ts, :], ACT.Abs_reciprocal_sqrt, bias=0.5)
 
-        def o_mul(cols):
-            nc.vector.tensor_tensor(res[:, :, cols], num[:, :, cols], rec[:, :, cols], ALU.mult)
-            nc.sync.dma_start(out_rows[:, :, cols], res[:, :, cols])
+        def o_square(c, ts):
+            nc.scalar.activation(rec[:, c, ts, :], root2[:, c, ts, :], ACT.Square)
 
-        def o_weave(cols):
+        def o_back(src, c, ts):
+            for t in range(ts.start, ts.stop):
+                nc.tensor.transpose(back[c][:, t, :], src[:, c, t, :], ident[:])
+
+        def o_mul(dst, src, c, ts):
+            nc.vector.tensor_tensor(dst[:, ts, :], src[:, ts, :], back[c][:, ts, :], ALU.mult)
+
+        def o_store(c):
+            nc.sync.dma_start(out_rows[:, :, chunk(c)], res[c][:])
+
+        def o_weave(c):
             nc.vector.tensor_copy(
-                ri[:, cols, :].rearrange("p (c i) t -> p c t i", i=4), res[:, :, cols].rearrange("p t (c i) -> p c t i", i=4)
+                ri[c][:].rearrange("p (c i) t -> p c t i", i=4), res[c][:].rearrange("p t (c i) -> p c t i", i=4)
             )
 
-        def o_quant(cols):
-            nc.vector.quantize_mx(oq[:, cols].bitcast(FP8X4), osc[:, cols], ri[:, cols, :].rearrange("p j t -> p (j t)"))
+        def o_quant(c):
+            cols = chunk(c)
+            nc.vector.quantize_mx(oq[:, cols].bitcast(FP8X4), osc[:, cols], ri[c][:].rearrange("p j t -> p (j t)"))
             nc.sync.dma_start(out_words[:, cols], oq[:, cols].bitcast(I32))
 
-        for cols in pieces:
-            o_rec(cols)
-        for i in range(len(pieces) + 2):
-            if i < len(pieces):
-                o_mul(pieces[i])
-            if 2 <= i:
-                o_quant(pieces[i - 2])
-            if 1 <= i <= len(pieces):
-                o_weave(pieces[i - 1])
+        every, low, high = slice(0, 4), slice(0, 2), slice(2, 4)
+        o_root(0, every)
+        o_back(root2, 0, every)
+        o_root(1, every)
+        o_root(2, every)
+        o_square(1, every)
+        o_back(rec, 1, every)
+        o_root(3, every)
+        o_square(2, every)
+        o_back(rec, 2, every)
+        o_square(3, every)
+        o_back(rec, 3, every)
+        o_mul(part, num[:, :, chunk(0)], 0, every)
+        o_mul(res[0], part, 0, every)
+        o_store(0)
+        o_mul(res[1], num[:, :, chunk(1)], 1, every)
+        o_store(1)
+        o_weave(0)
+        o_weave(1)
+        o_mul(res[2], num[:, :, chunk(2)], 2, every)
+        o_store(2)
+        o_quant(0)
+        o_quant(1)
+        o_weave(2)
+        o_mul(res[3], num[:, :, chunk(3)], 3, every)
+        o_store(3)
+        o_quant(2)
+        o_weave(3)
+        o_quant(3)
         for q in range(4):
             nc.scalar.dma_start(scale_rows(out_2, q), osc[32 * q : 32 * q + 4, :].bitcast(I32))

@@ -3,7 +3,7 @@ from contextlib import ExitStack
 import concourse.mybir as mybir
 from concourse.masks import make_identity
 
-FLOPS = 805306368
+FLOPS = 3 * 2 * 512 * 512 * 512
 
 F32 = mybir.dt.float32
 BF16 = mybir.dt.bfloat16
@@ -16,12 +16,16 @@ ACT = mybir.ActivationFunctionType
 ALU = mybir.AluOpType
 
 P = 128
+QUAD = 32
 PACK = 4
 T = 2048
 S = 512
 CH = 128
 NCH = S // CH
-HALF = 256
+HALF = S // 2
+SPARE = 16
+N1_SPANS = ((0, 2 * CH), (2 * CH, CH), (3 * CH, CH))
+ROOT_TWICE = 2
 
 
 def tile_picked_mixhnormkern_none_po_kernel(
@@ -37,7 +41,7 @@ def tile_picked_mixhnormkern_none_po_kernel(
             return dram[0].rearrange("p n t -> p (n t)").bitcast(I32)
 
         def scale_rows(dram, q):
-            return dram[0, 4 * q : 4 * q + 4, :].bitcast(I32)
+            return dram[0, PACK * q : PACK * (q + 1), :].bitcast(I32)
 
         def load_list(dram, name):
             lst = sb.tile([P, S // 16], U16, name=name)
@@ -47,156 +51,150 @@ def tile_picked_mixhnormkern_none_po_kernel(
         def entries(lst, start, count):
             return lst[:, start // 16 : (start + count) // 16]
 
-        offs_l = load_list(offs, "offs_l")
-        s1_raw = sb.tile([P, S], U8, name="s1_raw", align_bytes=64)
-        nc.sync.dma_start(s1_raw[:].bitcast(I32), w1_scales[0].bitcast(I32).unsqueeze(1).to_broadcast([16, 8, S // 4]))
-        xs = sb.tile([P, T], U8, name="xs", align_bytes=64)
-        for q in range(4):
-            nc.sync.dma_start(xs[32 * q : 32 * q + 32, :].bitcast(I32), scale_rows(x_scales, q).partition_broadcast(8))
-        w1_raw = sb.tile([P, S], U32, name="w1_raw", align_bytes=64)
-        nc.sync.dma_start(w1_raw[:].bitcast(I32), words_of(w1_words))
-        xw = sb.tile([P, T], U32, name="xw", align_bytes=64)
-        nc.sync.dma_start(xw[:].bitcast(I32), words_of(x_words))
-        one = sb.tile([P, 1], F32, name="one")
-        nc.gpsimd.memset(one[:], 1.0)
-        warm = sb.tile([P, 2], F32, name="warm")
-        nc.scalar.activation(warm[:, 0:1], one[:], ACT.Abs_reciprocal_sqrt)
-
-        hz_l = load_list(hz, "hz_l")
-        gain = sb.tile([P, PACK], F32, name="gain")
-        nc.sync.dma_start(gain[:], gn.rearrange("(p t) o -> p (t o)", t=PACK))
-        n1_l = load_list(n1, "n1_l")
-        s23_raw = sb.tile([P, S], U8, name="s23_raw", align_bytes=64)
-        nc.gpsimd.memset(s23_raw[:].bitcast(I32), 0)
-        for q in range(4):
-            nc.sync.dma_start(s23_raw[32 * q : 32 * q + 4, :].bitcast(I32), scale_rows(w2_scales, q))
-            nc.sync.dma_start(s23_raw[32 * q + 4 : 32 * q + 8, :].bitcast(I32), scale_rows(w3_scales, q))
-        w3_raw = sb.tile([P, S], U32, name="w3_raw", align_bytes=64)
-        nc.sync.dma_start(w3_raw[:].bitcast(I32), words_of(w3_words))
-        w2_raw = sb.tile([P, S], U32, name="w2_raw", align_bytes=64)
-        nc.sync.dma_start(w2_raw[:].bitcast(I32), words_of(w2_words))
-        n2_l = load_list(n2, "n2_l")
-        n3_l = load_list(n3, "n3_l")
+        def chunk(c):
+            return slice(c * CH, (c + 1) * CH)
 
         def deal(engine_copy, raw, dtype, name):
             dealt = sb.tile([P, S], dtype, name=name, align_bytes=64)
             engine_copy(dealt[:].rearrange("p (t m) -> p t m", t=PACK), raw[:].rearrange("p (m t) -> p t m", t=PACK))
             return dealt
 
-        s1_dealt = deal(nc.vector.tensor_copy, s1_raw, U8, "s1_dealt")
-        s1 = sb.tile([P, S], U8, name="s1", align_bytes=64)
-        for r in range(4):
-            nc.scalar.dma_start(s1[r:P:32, :].bitcast(I32), s1_dealt[8 * r : P : 32, :].bitcast(I32))
+        def woven(tile):
+            return tile[:].rearrange("p (c i) t -> p c t i", i=4)
+
+        def by_lines(ap):
+            return ap.rearrange("p t (c i) -> p c t i", i=4)
+
+        offs_l = load_list(offs, "offs_l")
+        scale_stage = sb.tile([P, S], U8, name="scale_stage", align_bytes=64)
+        nc.sync.dma_start(scale_stage[:].bitcast(I32), w1_scales[0].bitcast(I32).unsqueeze(1).to_broadcast([16, 8, S // 4]))
+        xs = sb.tile([P, T], U8, name="xs", align_bytes=64)
+        for q in range(PACK):
+            nc.sync.dma_start(xs[QUAD * q : QUAD * (q + 1), :].bitcast(I32), scale_rows(x_scales, q).partition_broadcast(8))
+        word_stage = sb.tile([P, S], U32, name="word_stage", align_bytes=64)
+        nc.sync.dma_start(word_stage[:].bitcast(I32), words_of(w1_words))
+        xw = sb.tile([P, T], U32, name="xw", align_bytes=64)
+        nc.sync.dma_start(xw[:].bitcast(I32), words_of(x_words))
+        hz_l = load_list(hz, "hz_l")
+        n1_l = load_list(n1, "n1_l")
+        n2_l = load_list(n2, "n2_l")
+        n3_l = load_list(n3, "n3_l")
+        gain = sb.tile([P, PACK], F32, name="gain")
+        nc.gpsimd.dma_start(gain[:], gn.rearrange("(p t) o -> p (t o)", t=PACK))
+
+        one = sb.tile([P, 1], F32, name="one")
+        nc.gpsimd.memset(one[:], 1.0)
+        warm = sb.tile([P, 2], F32, name="warm")
+        nc.scalar.activation(warm[:, 0:1], one[:], ACT.Abs_reciprocal_sqrt)
+
         ident = sb.tile([P, P], F32, name="ident")
         make_identity(nc, ident[:])
+
+        s1 = deal(nc.vector.tensor_copy, scale_stage, U8, "s1")
+        for r in range(1, PACK):
+            nc.sync.dma_start(s1[r:P:QUAD, :].bitcast(I32), s1[8 * r : P : QUAD, :].bitcast(I32))
+        w1 = deal(nc.scalar.copy, word_stage, U32, "w1")
+
+        for q in range(PACK):
+            nc.sync.dma_start(scale_stage[QUAD * q : QUAD * q + 4, :].bitcast(I32), scale_rows(w2_scales, q))
+            nc.sync.dma_start(scale_stage[QUAD * q + 4 : QUAD * q + 8, :].bitcast(I32), scale_rows(w3_scales, q))
+        nc.sync.dma_start(word_stage[:].bitcast(I32), words_of(w3_words))
+        w3 = deal(nc.gpsimd.tensor_copy, word_stage, U32, "w3")
+        s23 = deal(nc.gpsimd.tensor_copy, scale_stage, U8, "s23")
+        nc.sync.dma_start(word_stage[:].bitcast(I32), words_of(w2_words))
+        w2 = deal(nc.gpsimd.tensor_copy, word_stage, U32, "w2")
+
         gs = sb.tile([P, S], U8, name="gs", align_bytes=64)
         nc.vector.tensor_copy(gs[:], xs[:].indirect(offs_l[:]))
-        w1 = deal(nc.scalar.copy, w1_raw, U32, "w1")
         gw = sb.tile([P, S], U32, name="gw", align_bytes=64)
         for c in range(NCH):
-            nc.vector.tensor_copy(gw[:, c * CH : (c + 1) * CH], xw[:].indirect(entries(offs_l, c * CH, CH)))
+            nc.vector.tensor_copy(gw[:, chunk(c)], xw[:].indirect(entries(offs_l, c * CH, CH)))
 
-        hw = sb.tile([P, S], U32, name="hw", align_bytes=64)
         hs_raw = sb.tile([P, S], U8, name="hs_raw", align_bytes=64)
         nc.vector.tensor_copy(hs_raw[:], xs[:].indirect(hz_l[:]))
+        hw = sb.tile([P, S], U32, name="hw", align_bytes=64)
         nc.vector.tensor_copy(hw[:], xw[:].indirect(hz_l[:]))
         hs = sb.tile([P, S], U8, name="hs", align_bytes=64)
         nc.vector.tensor_copy(hs[:].bitcast(I32), hs_raw[:].bitcast(I32))
         for r in (2, 3):
-            nc.sync.dma_start(hs[r:P:32, :].bitcast(I32), hs_raw[16 + r : P : 32, :].bitcast(I32))
+            nc.sync.dma_start(hs[r:P:QUAD, :].bitcast(I32), hs_raw[16 + r : P : QUAD, :].bitcast(I32))
 
         y_ps = [ps.tile([P, PACK, CH], F32, name="y%d" % c) for c in range(NCH)]
         mag = sb.tile([P, PACK, S], F32, name="mag")
         root = sb.tile([P, PACK, S], F32, name="root")
         fac = [sb.tile([P, S], F32, name="fac%d" % t) for t in range(PACK)]
-        for c in range(NCH):
-            cols = slice(c * CH, (c + 1) * CH)
+
+        def y_chunk(c):
             for t in range(PACK):
                 nc.tensor.matmul_mx(
-                    y_ps[c][:, t, :], lhsT=w1[:, t * P : (t + 1) * P].bitcast(FP8X4), lhsT_scale=s1[:, t * P : (t + 1) * P],
-                    rhs=gw[:, cols].bitcast(FP8X4), rhs_scale=gs[:, cols], start=True, stop=True,
+                    y_ps[c][:, t, :], lhsT=w1[:, chunk(t)].bitcast(FP8X4), lhsT_scale=s1[:, chunk(t)],
+                    rhs=gw[:, chunk(c)].bitcast(FP8X4), rhs_scale=gs[:, chunk(c)], start=True, stop=True,
                 )
-            nc.scalar.activation(mag[:, :, cols], y_ps[c][:], ACT.Abs)
-            if c == 1:
-                half = slice(0, HALF)
-                nc.scalar.activation(root[:, :, half], mag[:, :, half], ACT.Abs_reciprocal_sqrt, bias=0.5)
-                for t in range(PACK):
-                    nc.vector.scalar_tensor_tensor(
-                        fac[t][:, half], root[:, t, half], gain[:, t : t + 1], root[:, t, half], ALU.mult, ALU.mult
-                    )
-        half = slice(HALF, S)
-        for t in range(PACK):
-            nc.scalar.activation(root[:, t, half], mag[:, t, half], ACT.Abs_reciprocal_sqrt, bias=0.5)
-            nc.vector.scalar_tensor_tensor(
-                fac[t][:, half], root[:, t, half], gain[:, t : t + 1], root[:, t, half], ALU.mult, ALU.mult
-            )
+            nc.scalar.activation(mag[:, :, chunk(c)], y_ps[c][:], ACT.Abs)
 
-        w3 = deal(nc.gpsimd.tensor_copy, w3_raw, U32, "w3")
-        s23 = deal(nc.gpsimd.tensor_copy, s23_raw, U8, "s23")
-        w2 = deal(nc.gpsimd.tensor_copy, w2_raw, U32, "w2")
+        def factor(t, cols):
+            nc.vector.scalar_tensor_tensor(fac[t][:, cols], root[:, t, cols], gain[:, t : t + 1], root[:, t, cols], ALU.mult, ALU.mult)
+
+        first, second = slice(0, HALF), slice(HALF, S)
+        for c in range(NCH // 2):
+            y_chunk(c)
+        nc.scalar.activation(root[:, :, first], mag[:, :, first], ACT.Abs_reciprocal_sqrt, bias=0.5)
+        for t in range(PACK):
+            factor(t, first)
+        for c in range(NCH // 2, NCH):
+            y_chunk(c)
+        for t in range(PACK):
+            nc.scalar.activation(root[:, t, second], mag[:, t, second], ACT.Abs_reciprocal_sqrt, bias=0.5)
+            factor(t, second)
 
         h_ps = [ps.tile([P, S], F32, name="h%d" % t) for t in range(PACK)]
         for t in range(PACK):
             nc.tensor.matmul_mx(
-                h_ps[t][:], lhsT=w3[:, t * P : (t + 1) * P].bitcast(FP8X4), lhsT_scale=s23[4:P, t * P : (t + 1) * P],
+                h_ps[t][:], lhsT=w3[:, chunk(t)].bitcast(FP8X4), lhsT_scale=s23[4:P, chunk(t)],
                 rhs=hw[:].bitcast(FP8X4), rhs_scale=hs[:], start=True, stop=False,
             )
 
-        spans = ((0, 256), (256, 128), (384, 128))
-        got = [sb.tile([P, PACK, count], F32, name="got%d" % start) for start, count in spans]
-        got_of = [got[0][:, :, :CH], got[0][:, :, CH:], got[1][:], got[2][:]]
+        got = [sb.tile([P, PACK, count], F32, name="got%d" % start) for start, count in N1_SPANS]
+        got_chunk = [tile[:, :, j : j + CH] for tile, span in zip(got, N1_SPANS) for j in range(0, span[1], CH)]
+        for tile, (start, count) in zip(got, N1_SPANS):
+            for t in range(PACK):
+                nc.scalar.activation(tile[:, t, :], fac[t][:].indirect(entries(n1_l, start, count)), ACT.Copy)
+        nc.scalar.activation(warm[:, 1:2], got[-1][:, PACK - 1, CH - 1 : CH], ACT.Tanh)
+
         zi = [sb.tile([P, CH, PACK], BF16, name="zi%d" % c, align_bytes=64) for c in range(NCH)]
         zq = sb.tile([P, S], U32, name="zq", align_bytes=64)
         zs = sb.tile([P, S], U8, name="zs", align_bytes=64)
 
-        def chunk(c):
-            return slice(c * CH, (c + 1) * CH)
-
         def z_mul(c):
-            nc.vector.tensor_tensor(
-                zi[c][:].rearrange("p (c i) t -> p c t i", i=4),
-                y_ps[c][:].rearrange("p t (c i) -> p c t i", i=4),
-                got_of[c].rearrange("p t (c i) -> p c t i", i=4),
-                ALU.mult,
-            )
+            nc.vector.tensor_tensor(woven(zi[c]), by_lines(y_ps[c][:]), by_lines(got_chunk[c]), ALU.mult)
 
         def z_quant(c):
-            cols = chunk(c)
-            nc.vector.quantize_mx(zq[:, cols].bitcast(FP8X4), zs[:, cols], zi[c][:].rearrange("p j t -> p (j t)"))
+            nc.vector.quantize_mx(zq[:, chunk(c)].bitcast(FP8X4), zs[:, chunk(c)], zi[c][:].rearrange("p j t -> p (j t)"))
             for t in range(PACK):
                 nc.tensor.matmul_mx(
-                    h_ps[t][:, cols], lhsT=w2[:, t * P : (t + 1) * P].bitcast(FP8X4), lhsT_scale=s23[:, t * P : (t + 1) * P],
-                    rhs=zq[:, cols].bitcast(FP8X4), rhs_scale=zs[:, cols], start=False, stop=(c == NCH - 1),
+                    h_ps[t][:, chunk(c)], lhsT=w2[:, chunk(t)].bitcast(FP8X4), lhsT_scale=s23[:, chunk(t)],
+                    rhs=zq[:, chunk(c)].bitcast(FP8X4), rhs_scale=zs[:, chunk(c)], start=False, stop=(c == NCH - 1),
                 )
 
-        for dst, (start, count) in zip(got, spans):
-            for t in range(PACK):
-                nc.scalar.activation(dst[:, t, :], fac[t][:].indirect(entries(n1_l, start, count)), ACT.Copy)
-        nc.scalar.activation(warm[:, 1:2], got[2][:, PACK - 1, CH - 1 : CH], ACT.Tanh)
+        for c in range(NCH + 1):
+            if c < NCH:
+                z_mul(c)
+            if c >= 1:
+                z_quant(c - 1)
 
-        z_mul(0)
-        z_mul(1)
-        z_quant(0)
-        z_mul(2)
-        z_quant(1)
-        z_mul(3)
-        z_quant(2)
-        z_quant(3)
-
-        h = [sb.tile([P, S + 16], F32, name="hrow%d" % t) for t in range(PACK)]
+        h = [sb.tile([P, S + SPARE], F32, name="hrow%d" % t) for t in range(PACK)]
         for t in range(PACK):
             nc.gpsimd.memset(h[t][:, S:], 0.0)
+            copy_out = nc.scalar.copy if t == 0 else nc.vector.tensor_copy
+            copy_out(h[t][:, :S], h_ps[t][:])
+
         dif = sb.tile([P, PACK, 2, S], F32, name="dif")
         sq = [sb.tile([P, 2, S], F32, name="sq%d" % t) for t in range(PACK)]
         near = [sb.tile([P, 2, S], F32, name="near%d" % t) for t in range(2)] + sq[:2]
         kr = sb.tile([P, PACK, 2, S], F32, name="kr")
         prod = sb.tile([P, PACK, 2, S], F32, name="prod")
         num = sb.tile([P, PACK, S], F32, name="num")
-        for t in range(PACK):
-            if t == 0:
-                nc.scalar.copy(h[t][:, :S], h_ps[t][:])
-            else:
-                nc.vector.tensor_copy(h[t][:, :S], h_ps[t][:])
+        ksum_ps = y_ps
 
         def fetch(t):
             for a, lst in enumerate((n2_l, n3_l)):
@@ -205,16 +203,16 @@ def tile_picked_mixhnormkern_none_po_kernel(
         def sub(t, a):
             nc.vector.tensor_tensor(dif[:, t, a, :], near[t][:, a, :], h_ps[t][:], ALU.subtract)
 
-        def square(t):
-            nc.vector.tensor_tensor(sq[t][:], dif[:, t, :, :], dif[:, t, :, :], ALU.mult)
+        def square(t, sides):
+            nc.vector.tensor_tensor(sq[t][:, sides, :], dif[:, t, sides, :], dif[:, t, sides, :], ALU.mult)
 
-        def expo(t):
+        def weights(t):
             nc.scalar.activation(kr[:, t, :, :], sq[t][:], ACT.Exp, scale=-0.5)
-
-        def ksums(t):
             for c in range(NCH):
                 for a in range(2):
-                    nc.tensor.matmul(y_ps[c][:, t, :], lhsT=kr[:, t, a, chunk(c)], rhs=ident[:], is_transpose=True, start=(a == 0), stop=(a == 1))
+                    nc.tensor.matmul(
+                        ksum_ps[c][:, t, :], lhsT=kr[:, t, a, chunk(c)], rhs=ident[:], is_transpose=True, start=(a == 0), stop=(a == 1)
+                    )
 
         def prods(t):
             nc.vector.tensor_tensor(prod[:, t, :, :], kr[:, t, :, :], near[t][:], ALU.mult)
@@ -222,113 +220,66 @@ def tile_picked_mixhnormkern_none_po_kernel(
         def nums(t):
             nc.vector.tensor_tensor(num[:, t, :], prod[:, t, 0, :], prod[:, t, 1, :], ALU.add)
 
-        def half_square(t, a):
-            nc.vector.tensor_tensor(sq[t][:, a, :], dif[:, t, a, :], dif[:, t, a, :], ALU.mult)
-
-        def half_expo(t, a):
-            nc.scalar.activation(kr[:, t, a, :], sq[t][:, a, :], ACT.Exp, scale=-0.5)
-
-        fetch(0)
-        sub(0, 0)
-        half_square(0, 0)
-        sub(0, 1)
-        half_square(0, 1)
-        fetch(1)
-        expo(0)
-        ksums(0)
-        sub(1, 0)
-        sub(1, 1)
-        square(1)
-        fetch(2)
-        expo(1)
-        ksums(1)
-        prods(0)
-        sub(2, 0)
-        sub(2, 1)
-        square(2)
-        fetch(3)
-        expo(2)
-        ksums(2)
-        sub(3, 0)
-        prods(1)
-        sub(3, 1)
-        half_square(3, 0)
-        half_square(3, 1)
-        half_expo(3, 0)
-        half_expo(3, 1)
-        ksums(3)
-        nums(0)
-        prods(2)
-        nums(1)
-        prods(3)
-        nums(2)
-        nums(3)
+        last = PACK - 1
+        for t in range(PACK):
+            fetch(t)
+            if t >= 1:
+                weights(t - 1)
+            if t >= 2:
+                prods(t - 2)
+            if t == 0:
+                for a in range(2):
+                    sub(t, a)
+                    square(t, slice(a, a + 1))
+            else:
+                for a in range(2):
+                    sub(t, a)
+                if t < last:
+                    square(t, slice(0, 2))
+        for a in range(2):
+            nc.scalar.activation(sq[last][:, a, :], dif[:, last, a, :], ACT.Square)
+        weights(last)
+        for t in range(PACK):
+            if t < 2:
+                nums(t)
+                prods(t + 2)
+            else:
+                nums(t)
 
         root2 = sb.tile([P, NCH, PACK, P], F32, name="root2")
-        rec = sb.tile([P, NCH, PACK, P], F32, name="rec")
-        part = sb.tile([P, PACK, CH], F32, name="part")
+        rec = sb.tile([P, NCH - ROOT_TWICE, PACK, P], F32, name="rec")
+        part = sb.tile([P, ROOT_TWICE, PACK, CH], F32, name="part")
         res = [sb.tile([P, PACK, CH], F32, name="res%d" % c) for c in range(NCH)]
         ri = [sb.tile([P, CH, PACK], BF16, name="ri%d" % c, align_bytes=64) for c in range(NCH)]
         oq = sb.tile([P, S], U32, name="oq", align_bytes=64)
         osc = sb.tile([P, S], U8, name="osc", align_bytes=64)
         out_rows = out_0.rearrange("(p t) j -> p t j", t=PACK)
         out_words = words_of(out_1)
-        back = [h_ps[c][:].rearrange("p (t j) -> p t j", t=PACK) for c in range(NCH)]
+        back_ps = [bank[:].rearrange("p (t j) -> p t j", t=PACK) for bank in h_ps]
 
-        def o_root(c, ts):
-            nc.scalar.activation(root2[:, c, ts, :], y_ps[c][:, ts, :], ACT.Abs_reciprocal_sqrt, bias=0.5)
+        def turn_back(src, c):
+            for t in range(PACK):
+                nc.tensor.transpose(back_ps[c][:, t, :], src[:, t, :], ident[:])
 
-        def o_square(c, ts):
-            nc.scalar.activation(rec[:, c, ts, :], root2[:, c, ts, :], ACT.Square)
-
-        def o_back(src, c, ts):
-            for t in range(ts.start, ts.stop):
-                nc.tensor.transpose(back[c][:, t, :], src[:, c, t, :], ident[:])
-
-        def o_mul(dst, src, c, ts):
-            nc.vector.tensor_tensor(dst[:, ts, :], src[:, ts, :], back[c][:, ts, :], ALU.mult)
-
-        def o_store(c):
+        for c in range(NCH):
+            nc.scalar.activation(root2[:, c, :, :], ksum_ps[c][:], ACT.Abs_reciprocal_sqrt, bias=0.5)
+            if c < ROOT_TWICE:
+                turn_back(root2[:, c, :, :], c)
+                nc.vector.tensor_tensor(part[:, c, :, :], num[:, :, chunk(c)], back_ps[c], ALU.mult)
+        for c in range(ROOT_TWICE, NCH):
+            nc.scalar.activation(rec[:, c - ROOT_TWICE, :, :], root2[:, c, :, :], ACT.Square)
+            turn_back(rec[:, c - ROOT_TWICE, :, :], c)
+        for c in range(NCH):
+            src = part[:, c, :, :] if c < ROOT_TWICE else num[:, :, chunk(c)]
+            nc.vector.tensor_tensor(res[c][:], src, back_ps[c], ALU.mult)
             nc.sync.dma_start(out_rows[:, :, chunk(c)], res[c][:])
-
-        def o_weave(c):
-            nc.vector.tensor_copy(
-                ri[c][:].rearrange("p (c i) t -> p c t i", i=4), res[c][:].rearrange("p t (c i) -> p c t i", i=4)
-            )
-
-        def o_quant(c):
-            cols = chunk(c)
-            nc.vector.quantize_mx(oq[:, cols].bitcast(FP8X4), osc[:, cols], ri[c][:].rearrange("p j t -> p (j t)"))
-            nc.sync.dma_start(out_words[:, cols], oq[:, cols].bitcast(I32))
-
-        every, low, high = slice(0, 4), slice(0, 2), slice(2, 4)
-        o_root(0, every)
-        o_back(root2, 0, every)
-        o_root(1, every)
-        o_root(2, every)
-        o_square(1, every)
-        o_back(rec, 1, every)
-        o_root(3, every)
-        o_square(2, every)
-        o_back(rec, 2, every)
-        o_square(3, every)
-        o_back(rec, 3, every)
-        o_mul(part, num[:, :, chunk(0)], 0, every)
-        o_mul(res[0], part, 0, every)
-        o_store(0)
-        o_mul(res[1], num[:, :, chunk(1)], 1, every)
-        o_store(1)
-        o_weave(0)
-        o_weave(1)
-        o_mul(res[2], num[:, :, chunk(2)], 2, every)
-        o_store(2)
-        o_quant(0)
-        o_quant(1)
-        o_weave(2)
-        o_mul(res[3], num[:, :, chunk(3)], 3, every)
-        o_store(3)
-        o_quant(2)
-        o_weave(3)
-        o_quant(3)
-        for q in range(4):
-            nc.scalar.dma_start(scale_rows(out_2, q), osc[32 * q : 32 * q + 4, :].bitcast(I32))
+        for c in range(NCH):
+            round_copy = nc.scalar.copy if c < NCH - 1 else nc.vector.tensor_copy
+            round_copy(woven(ri[c]), by_lines(res[c][:]))
+            nc.vector.quantize_mx(oq[:, chunk(c)].bitcast(FP8X4), osc[:, chunk(c)], ri[c][:].rearrange("p j t -> p (j t)"))
+            if c % 2 == 1:
+                cols = slice((c - 1) * CH, (c + 1) * CH)
+                nc.sync.dma_start(out_words[:, cols], oq[:, cols].bitcast(I32))
+        for q in range(PACK):
+            queue = nc.scalar if q % 2 == 0 else nc.sync
+            queue.dma_start(scale_rows(out_2, q), osc[QUAD * q : QUAD * q + 4, :].bitcast(I32))

@@ -56,7 +56,7 @@ def tile_picked_mixhnormkern_none_po_kernel(
 
         def deal(engine_copy, raw, dtype, name):
             dealt = sb.tile([P, S], dtype, name=name, align_bytes=64)
-            engine_copy(dealt[:].rearrange("p (t m) -> p t m", t=PACK), raw[:].rearrange("p (m t) -> p t m", t=PACK))
+            engine_copy(dealt[:].rearrange("p (t m) -> p t m", t=PACK), raw.rearrange("p (m t) -> p t m", t=PACK))
             return dealt
 
         def woven(tile):
@@ -90,19 +90,19 @@ def tile_picked_mixhnormkern_none_po_kernel(
         ident = sb.tile([P, P], F32, name="ident")
         make_identity(nc, ident[:])
 
-        s1 = deal(nc.vector.tensor_copy, scale_stage, U8, "s1")
+        s1 = deal(nc.vector.tensor_copy, scale_stage[:], U8, "s1")
         for r in range(1, PACK):
             nc.sync.dma_start(s1[r:P:QUAD, :].bitcast(I32), s1[8 * r : P : QUAD, :].bitcast(I32))
-        w1 = deal(nc.scalar.copy, word_stage, U32, "w1")
+        w1 = deal(nc.scalar.copy, word_stage[:], U32, "w1")
 
         for q in range(PACK):
             nc.sync.dma_start(scale_stage[QUAD * q : QUAD * q + 4, :].bitcast(I32), scale_rows(w2_scales, q))
             nc.sync.dma_start(scale_stage[QUAD * q + 4 : QUAD * q + 8, :].bitcast(I32), scale_rows(w3_scales, q))
-        nc.sync.dma_start(word_stage[:].bitcast(I32), words_of(w3_words))
-        w3 = deal(nc.gpsimd.tensor_copy, word_stage, U32, "w3")
-        s23 = deal(nc.gpsimd.tensor_copy, scale_stage, U8, "s23")
-        nc.sync.dma_start(word_stage[:].bitcast(I32), words_of(w2_words))
-        w2 = deal(nc.gpsimd.tensor_copy, word_stage, U32, "w2")
+        w23_raw = sb.tile([P, 2 * S], U32, name="word_stage", align_bytes=64)
+        nc.sync.dma_start(w23_raw[:, :S].bitcast(I32), words_of(w3_words))
+        nc.sync.dma_start(w23_raw[:, S:].bitcast(I32), words_of(w2_words))
+        w3 = deal(nc.gpsimd.tensor_copy, w23_raw[:, :S], U32, "w3")
+        s23 = deal(nc.gpsimd.tensor_copy, scale_stage[:], U8, "s23")
 
         gs = sb.tile([P, S], U8, name="gs", align_bytes=64)
         nc.vector.tensor_copy(gs[:], xs[:].indirect(offs_l[:]))
@@ -121,7 +121,7 @@ def tile_picked_mixhnormkern_none_po_kernel(
 
         y_ps = [ps.tile([P, PACK, CH], F32, name="y%d" % c) for c in range(NCH)]
         mag = sb.tile([P, PACK, S], F32, name="mag")
-        root = sb.tile([P, PACK, S], F32, name="root")
+        root = sb.tile([P, PACK, S], F32, name="root", align_bytes=64)
         fac = [sb.tile([P, S], F32, name="fac%d" % t) for t in range(PACK)]
 
         def y_chunk(c):
@@ -143,9 +143,12 @@ def tile_picked_mixhnormkern_none_po_kernel(
             factor(t, first)
         for c in range(NCH // 2, NCH):
             y_chunk(c)
-        for t in range(PACK):
-            nc.scalar.activation(root[:, t, second], mag[:, t, second], ACT.Abs_reciprocal_sqrt, bias=0.5)
-            factor(t, second)
+        for tiles in (slice(0, 2), slice(2, PACK)):
+            nc.scalar.activation(root[:, tiles, second], mag[:, tiles, second], ACT.Abs_reciprocal_sqrt, bias=0.5)
+            for t in range(tiles.start, tiles.stop):
+                factor(t, second)
+
+        w2 = deal(nc.vector.tensor_copy, w23_raw[:, S:], U32, "root")
 
         h_ps = [ps.tile([P, S], F32, name="h%d" % t) for t in range(PACK)]
         for t in range(PACK):
@@ -161,7 +164,7 @@ def tile_picked_mixhnormkern_none_po_kernel(
                 nc.scalar.activation(tile[:, t, :], fac[t][:].indirect(entries(n1_l, start, count)), ACT.Copy)
         nc.scalar.activation(warm[:, 1:2], got[-1][:, PACK - 1, CH - 1 : CH], ACT.Tanh)
 
-        zi = [sb.tile([P, CH, PACK], BF16, name="zi%d" % c, align_bytes=64) for c in range(NCH)]
+        zi = [sb.tile([P, CH, PACK], BF16, name="zi%d" % c if c else "word_stage", align_bytes=64) for c in range(NCH)]
         zq = sb.tile([P, S], U32, name="zq", align_bytes=64)
         zs = sb.tile([P, S], U8, name="zs", align_bytes=64)
 
@@ -225,8 +228,6 @@ def tile_picked_mixhnormkern_none_po_kernel(
             fetch(t)
             if t >= 1:
                 weights(t - 1)
-            if t >= 2:
-                prods(t - 2)
             if t == 0:
                 for a in range(2):
                     sub(t, a)
@@ -234,6 +235,8 @@ def tile_picked_mixhnormkern_none_po_kernel(
             else:
                 for a in range(2):
                     sub(t, a)
+                if t >= 2:
+                    prods(t - 2)
                 if t < last:
                     square(t, slice(0, 2))
         for a in range(2):

from contextlib import ExitStack

import concourse.mybir as mybir
from concourse.masks import make_identity

FLOPS = 3 * 2 * 512 * 512 * 512

F32 = mybir.dt.float32
BF16 = mybir.dt.bfloat16
I32 = mybir.dt.int32
U32 = mybir.dt.uint32
U16 = mybir.dt.uint16
U8 = mybir.dt.uint8
FP8X4 = mybir.dt.float8_e4m3fn_x4
ACT = mybir.ActivationFunctionType
ALU = mybir.AluOpType

P = 128
QUAD = 32
PACK = 4
T = 2048
S = 512
CH = 128
NCH = S // CH
HALF = S // 2
SPARE = 16
N1_SPANS = ((0, 2 * CH), (2 * CH, CH), (3 * CH, CH))
ROOT_TWICE = 2


def tile_picked_mixhnormkern_none_po_kernel(
    tc, x_words, x_scales, w1_words, w1_scales, gn, w2_words, w2_scales, w3_words, w3_scales,
    offs, n1, hz, n2, n3, out_0, out_1, out_2,
):
    nc = tc.nc
    with ExitStack() as ctx:
        sb = ctx.enter_context(tc.tile_pool(name="sb", bufs=1))
        ps = ctx.enter_context(tc.psum_pool(name="ps", bufs=1))

        def words_of(dram):
            return dram[0].rearrange("p n t -> p (n t)").bitcast(I32)

        def scale_rows(dram, q):
            return dram[0, PACK * q : PACK * (q + 1), :].bitcast(I32)

        def load_list(dram, name):
            lst = sb.tile([P, S // 16], U16, name=name)
            nc.sync.dma_start(lst[:], dram)
            return lst

        def entries(lst, start, count):
            return lst[:, start // 16 : (start + count) // 16]

        def chunk(c):
            return slice(c * CH, (c + 1) * CH)

        def deal(engine_copy, raw, dtype, name):
            dealt = sb.tile([P, S], dtype, name=name, align_bytes=64)
            engine_copy(dealt[:].rearrange("p (t m) -> p t m", t=PACK), raw.rearrange("p (m t) -> p t m", t=PACK))
            return dealt

        def woven(tile):
            return tile[:].rearrange("p (c i) t -> p c t i", i=4)

        def by_lines(ap):
            return ap.rearrange("p t (c i) -> p c t i", i=4)

        offs_l = load_list(offs, "offs_l")
        scale_stage = sb.tile([P, S], U8, name="scale_stage", align_bytes=64)
        nc.sync.dma_start(scale_stage[:].bitcast(I32), w1_scales[0].bitcast(I32).unsqueeze(1).to_broadcast([16, 8, S // 4]))
        xs = sb.tile([P, T], U8, name="xs", align_bytes=64)
        for q in range(PACK):
            nc.sync.dma_start(xs[QUAD * q : QUAD * (q + 1), :].bitcast(I32), scale_rows(x_scales, q).partition_broadcast(8))
        word_stage = sb.tile([P, S], U32, name="word_stage", align_bytes=64)
        nc.sync.dma_start(word_stage[:].bitcast(I32), words_of(w1_words))
        xw = sb.tile([P, T], U32, name="xw", align_bytes=64)
        nc.sync.dma_start(xw[:].bitcast(I32), words_of(x_words))
        hz_l = load_list(hz, "hz_l")
        n1_l = load_list(n1, "n1_l")
        n2_l = load_list(n2, "n2_l")
        n3_l = load_list(n3, "n3_l")
        gain = sb.tile([P, PACK], F32, name="gain")
        nc.gpsimd.dma_start(gain[:], gn.rearrange("(p t) o -> p (t o)", t=PACK))

        one = sb.tile([P, 1], F32, name="one")
        nc.gpsimd.memset(one[:], 1.0)
        warm = sb.tile([P, 2], F32, name="warm")
        nc.scalar.activation(warm[:, 0:1], one[:], ACT.Abs_reciprocal_sqrt)

        ident = sb.tile([P, P], F32, name="ident")
        make_identity(nc, ident[:])

        s1 = deal(nc.vector.tensor_copy, scale_stage[:], U8, "s1")
        for r in range(1, PACK):
            nc.sync.dma_start(s1[r:P:QUAD, :].bitcast(I32), s1[8 * r : P : QUAD, :].bitcast(I32))
        w1 = deal(nc.scalar.copy, word_stage[:], U32, "w1")

        for q in range(PACK):
            nc.sync.dma_start(scale_stage[QUAD * q : QUAD * q + 4, :].bitcast(I32), scale_rows(w2_scales, q))
            nc.sync.dma_start(scale_stage[QUAD * q + 4 : QUAD * q + 8, :].bitcast(I32), scale_rows(w3_scales, q))
        w23_raw = sb.tile([P, 2 * S], U32, name="word_stage", align_bytes=64)
        nc.sync.dma_start(w23_raw[:, :S].bitcast(I32), words_of(w3_words))
        nc.sync.dma_start(w23_raw[:, S:].bitcast(I32), words_of(w2_words))
        w3 = deal(nc.gpsimd.tensor_copy, w23_raw[:, :S], U32, "w3")
        s23 = deal(nc.gpsimd.tensor_copy, scale_stage[:], U8, "s23")

        gs = sb.tile([P, S], U8, name="gs", align_bytes=64)
        nc.vector.tensor_copy(gs[:], xs[:].indirect(offs_l[:]))
        gw = sb.tile([P, S], U32, name="gw", align_bytes=64)
        for c in range(NCH):
            nc.vector.tensor_copy(gw[:, chunk(c)], xw[:].indirect(entries(offs_l, c * CH, CH)))

        hs_raw = sb.tile([P, S], U8, name="hs_raw", align_bytes=64)
        nc.vector.tensor_copy(hs_raw[:], xs[:].indirect(hz_l[:]))
        hw = sb.tile([P, S], U32, name="hw", align_bytes=64)
        nc.vector.tensor_copy(hw[:], xw[:].indirect(hz_l[:]))
        hs = sb.tile([P, S], U8, name="hs", align_bytes=64)
        nc.vector.tensor_copy(hs[:].bitcast(I32), hs_raw[:].bitcast(I32))
        for r in (2, 3):
            nc.sync.dma_start(hs[r:P:QUAD, :].bitcast(I32), hs_raw[16 + r : P : QUAD, :].bitcast(I32))

        y_ps = [ps.tile([P, PACK, CH], F32, name="y%d" % c) for c in range(NCH)]
        mag = sb.tile([P, PACK, S], F32, name="mag")
        root = sb.tile([P, PACK, S], F32, name="root", align_bytes=64)
        fac = [sb.tile([P, S], F32, name="fac%d" % t) for t in range(PACK)]

        def y_chunk(c):
            for t in range(PACK):
                nc.tensor.matmul_mx(
                    y_ps[c][:, t, :], lhsT=w1[:, chunk(t)].bitcast(FP8X4), lhsT_scale=s1[:, chunk(t)],
                    rhs=gw[:, chunk(c)].bitcast(FP8X4), rhs_scale=gs[:, chunk(c)], start=True, stop=True,
                )
            nc.scalar.activation(mag[:, :, chunk(c)], y_ps[c][:], ACT.Abs)

        def factor(t, cols):
            nc.vector.scalar_tensor_tensor(fac[t][:, cols], root[:, t, cols], gain[:, t : t + 1], root[:, t, cols], ALU.mult, ALU.mult)

        first, second = slice(0, HALF), slice(HALF, S)
        for c in range(NCH // 2):
            y_chunk(c)
        nc.scalar.activation(root[:, :, first], mag[:, :, first], ACT.Abs_reciprocal_sqrt, bias=0.5)
        for t in range(PACK):
            factor(t, first)
        for c in range(NCH // 2, NCH):
            y_chunk(c)
        for tiles in (slice(0, 2), slice(2, PACK)):
            nc.scalar.activation(root[:, tiles, second], mag[:, tiles, second], ACT.Abs_reciprocal_sqrt, bias=0.5)
            for t in range(tiles.start, tiles.stop):
                factor(t, second)

        w2 = deal(nc.vector.tensor_copy, w23_raw[:, S:], U32, "root")

        h_ps = [ps.tile([P, S], F32, name="h%d" % t) for t in range(PACK)]
        for t in range(PACK):
            nc.tensor.matmul_mx(
                h_ps[t][:], lhsT=w3[:, chunk(t)].bitcast(FP8X4), lhsT_scale=s23[4:P, chunk(t)],
                rhs=hw[:].bitcast(FP8X4), rhs_scale=hs[:], start=True, stop=False,
            )

        got = [sb.tile([P, PACK, count], F32, name="got%d" % start) for start, count in N1_SPANS]
        got_chunk = [tile[:, :, j : j + CH] for tile, span in zip(got, N1_SPANS) for j in range(0, span[1], CH)]
        for tile, (start, count) in zip(got, N1_SPANS):
            for t in range(PACK):
                nc.scalar.activation(tile[:, t, :], fac[t][:].indirect(entries(n1_l, start, count)), ACT.Copy)
        nc.scalar.activation(warm[:, 1:2], got[-1][:, PACK - 1, CH - 1 : CH], ACT.Tanh)

        zi = [sb.tile([P, CH, PACK], BF16, name="zi%d" % c if c else "word_stage", align_bytes=64) for c in range(NCH)]
        zq = sb.tile([P, S], U32, name="zq", align_bytes=64)
        zs = sb.tile([P, S], U8, name="zs", align_bytes=64)

        def z_mul(c):
            nc.vector.tensor_tensor(woven(zi[c]), by_lines(y_ps[c][:]), by_lines(got_chunk[c]), ALU.mult)

        def z_quant(c):
            nc.vector.quantize_mx(zq[:, chunk(c)].bitcast(FP8X4), zs[:, chunk(c)], zi[c][:].rearrange("p j t -> p (j t)"))
            for t in range(PACK):
                nc.tensor.matmul_mx(
                    h_ps[t][:, chunk(c)], lhsT=w2[:, chunk(t)].bitcast(FP8X4), lhsT_scale=s23[:, chunk(t)],
                    rhs=zq[:, chunk(c)].bitcast(FP8X4), rhs_scale=zs[:, chunk(c)], start=False, stop=(c == NCH - 1),
                )

        for c in range(NCH + 1):
            if c < NCH:
                z_mul(c)
            if c >= 1:
                z_quant(c - 1)

        h = [sb.tile([P, S + SPARE], F32, name="hrow%d" % t) for t in range(PACK)]
        for t in range(PACK):
            nc.gpsimd.memset(h[t][:, S:], 0.0)
            copy_out = nc.scalar.copy if t == 0 else nc.vector.tensor_copy
            copy_out(h[t][:, :S], h_ps[t][:])

        dif = sb.tile([P, PACK, 2, S], F32, name="dif")
        sq = [sb.tile([P, 2, S], F32, name="sq%d" % t) for t in range(PACK)]
        near = [sb.tile([P, 2, S], F32, name="near%d" % t) for t in range(2)] + sq[:2]
        kr = sb.tile([P, PACK, 2, S], F32, name="kr")
        prod = sb.tile([P, PACK, 2, S], F32, name="prod")
        num = sb.tile([P, PACK, S], F32, name="num")
        ksum_ps = y_ps

        def fetch(t):
            for a, lst in enumerate((n2_l, n3_l)):
                nc.scalar.activation(near[t][:, a, :], h[t][:].indirect(lst[:]), ACT.Copy)

        def sub(t, a):
            nc.vector.tensor_tensor(dif[:, t, a, :], near[t][:, a, :], h_ps[t][:], ALU.subtract)

        def square(t, sides):
            nc.vector.tensor_tensor(sq[t][:, sides, :], dif[:, t, sides, :], dif[:, t, sides, :], ALU.mult)

        def weights(t):
            nc.scalar.activation(kr[:, t, :, :], sq[t][:], ACT.Exp, scale=-0.5)
            for c in range(NCH):
                for a in range(2):
                    nc.tensor.matmul(
                        ksum_ps[c][:, t, :], lhsT=kr[:, t, a, chunk(c)], rhs=ident[:], is_transpose=True, start=(a == 0), stop=(a == 1)
                    )

        def prods(t):
            nc.vector.tensor_tensor(prod[:, t, :, :], kr[:, t, :, :], near[t][:], ALU.mult)

        def nums(t):
            nc.vector.tensor_tensor(num[:, t, :], prod[:, t, 0, :], prod[:, t, 1, :], ALU.add)

        last = PACK - 1
        for t in range(PACK):
            fetch(t)
            if t >= 1:
                weights(t - 1)
            if t == 0:
                for a in range(2):
                    sub(t, a)
                    square(t, slice(a, a + 1))
            else:
                for a in range(2):
                    sub(t, a)
                if t >= 2:
                    prods(t - 2)
                if t < last:
                    square(t, slice(0, 2))
        for a in range(2):
            nc.scalar.activation(sq[last][:, a, :], dif[:, last, a, :], ACT.Square)
        weights(last)
        for t in range(PACK):
            if t < 2:
                nums(t)
                prods(t + 2)
            else:
                nums(t)

        root2 = sb.tile([P, NCH, PACK, P], F32, name="root2")
        rec = sb.tile([P, NCH - ROOT_TWICE, PACK, P], F32, name="rec")
        part = sb.tile([P, ROOT_TWICE, PACK, CH], F32, name="part")
        res = [sb.tile([P, PACK, CH], F32, name="res%d" % c) for c in range(NCH)]
        ri = [sb.tile([P, CH, PACK], BF16, name="ri%d" % c, align_bytes=64) for c in range(NCH)]
        oq = sb.tile([P, S], U32, name="oq", align_bytes=64)
        osc = sb.tile([P, S], U8, name="osc", align_bytes=64)
        out_rows = out_0.rearrange("(p t) j -> p t j", t=PACK)
        out_words = words_of(out_1)
        back_ps = [bank[:].rearrange("p (t j) -> p t j", t=PACK) for bank in h_ps]

        def turn_back(src, c):
            for t in range(PACK):
                nc.tensor.transpose(back_ps[c][:, t, :], src[:, t, :], ident[:])

        for c in range(NCH):
            nc.scalar.activation(root2[:, c, :, :], ksum_ps[c][:], ACT.Abs_reciprocal_sqrt, bias=0.5)
            if c < ROOT_TWICE:
                turn_back(root2[:, c, :, :], c)
                nc.vector.tensor_tensor(part[:, c, :, :], num[:, :, chunk(c)], back_ps[c], ALU.mult)
        for c in range(ROOT_TWICE, NCH):
            nc.scalar.activation(rec[:, c - ROOT_TWICE, :, :], root2[:, c, :, :], ACT.Square)
            turn_back(rec[:, c - ROOT_TWICE, :, :], c)
        for c in range(NCH):
            src = part[:, c, :, :] if c < ROOT_TWICE else num[:, :, chunk(c)]
            nc.vector.tensor_tensor(res[c][:], src, back_ps[c], ALU.mult)
            nc.sync.dma_start(out_rows[:, :, chunk(c)], res[c][:])
        for c in range(NCH):
            round_copy = nc.scalar.copy if c < NCH - 1 else nc.vector.tensor_copy
            round_copy(woven(ri[c]), by_lines(res[c][:]))
            nc.vector.quantize_mx(oq[:, chunk(c)].bitcast(FP8X4), osc[:, chunk(c)], ri[c][:].rearrange("p j t -> p (j t)"))
            if c % 2 == 1:
                cols = slice((c - 1) * CH, (c + 1) * CH)
                nc.sync.dma_start(out_words[:, cols], oq[:, cols].bitcast(I32))
        for q in range(PACK):
            queue = nc.scalar if q % 2 == 0 else nc.sync
            queue.dma_start(scale_rows(out_2, q), osc[QUAD * q : QUAD * q + 4, :].bitcast(I32))
